import numpy as np
import ml_dtypes


def mxq(x, axis, fmt="e4m3"):
    dtype, down = {"e4m3": (ml_dtypes.float8_e4m3fn, 7), "e5m2": (ml_dtypes.float8_e5m2, 14)}[fmt]
    v = np.moveaxis(np.asarray(x, np.float32).astype(ml_dtypes.bfloat16).astype(np.float64), axis, -1)
    blocks = v.reshape(v.shape[:-1] + (-1, 32))
    amax = np.abs(blocks).max(-1, keepdims=True)
    byte = np.maximum(np.where(amax > 0, np.frexp(amax)[1] - 1 + 127, 0) - down, 1)
    scale = np.exp2(byte - 127.0)
    codes = (blocks / scale).astype(np.float32).astype(dtype).astype(np.float64)
    return np.moveaxis((codes * scale).reshape(v.shape), -1, axis)


WIDE = False


def mx_kscale(k):
    if not WIDE:
        return np.ones(k)
    levels = np.array([10, -10, 5, -5, 0])
    if k % 512:
        return np.exp2(np.random.permutation(np.resize(levels, k // 32))).repeat(32)
    a = np.empty((k // 512, 16))
    for p in range(k // 512):
        a[p, :8] = np.random.permutation(np.resize(levels, 8))
        for g in range(8):
            far = levels[np.abs(levels - a[p, g]) >= 10]
            a[p, g + 8] = far[np.random.randint(len(far))]
    return np.exp2(a.ravel()).repeat(32)


def f64(x):
    return np.asarray(x).astype(np.float64)


def striped(idx):
    return np.tile(idx.reshape(-1, 16).T, (8, 1)).astype(np.uint16)


def unstriped(offs):
    return offs[:16].T.reshape(-1).astype(np.int64)


def striped8(idx):
    return np.concatenate([x.reshape(-1, 16).T for x in idx]).astype(np.uint16)


def runs(offs, k):
    lists = np.stack([offs[16 * r : 16 * r + 16].T.reshape(-1) for r in range(8)]).astype(np.int64)
    return lists[np.arange(k) % 512 // 64]


def pack_weight(w):
    k, n = w.shape
    w = f64(np.asarray(w, np.float32).astype(ml_dtypes.bfloat16)).reshape(k // 32, 32, n)
    amax = np.abs(w).max(1)
    byte = np.clip(np.where(amax > 0, np.frexp(amax)[1] - 1 + 127 - 7, 1), 1, 254)
    scaled = (w * np.exp2(127.0 - byte)[:, None, :]).reshape(k, n).astype(np.float32)
    words = np.ascontiguousarray(scaled.reshape(k // 512, 128, 4, n).transpose(0, 1, 3, 2)).astype(ml_dtypes.float8_e4m3fn).view(np.uint8)
    return words, np.ascontiguousarray(byte.astype(np.uint8).reshape(k // 512, 16, n))


def unpack_weight(words, scales):
    g, p, n, _ = words.shape
    vals = np.ascontiguousarray(words).view(ml_dtypes.float8_e4m3fn).astype(np.float64) * np.repeat(np.exp2(scales.astype(np.float64) - 127.0), 8, axis=1)[..., None]
    return vals.transpose(0, 1, 3, 2).reshape(g * 512, n)


def sigmoid(v):
    return 1.0 / (1.0 + np.exp(-np.maximum(v, -700.0)))

def planes(y):
    n, m = y.shape
    v = y.astype(np.float32).astype(ml_dtypes.bfloat16).astype(np.float64).reshape(n // 32, 32, m)
    top = np.abs(v).max(1)
    byte = np.clip(np.where(top > 0, np.frexp(top)[1] - 1 + 127 - 7, 1), 1, 254)
    codes = (v * np.exp2(127.0 - byte)[:, None, :]).reshape(n, m).astype(np.float32).astype(ml_dtypes.float8_e4m3fn).view(np.uint8)
    words = codes.reshape(n // 512, 128, 4, m).transpose(0, 1, 3, 2)
    return np.ascontiguousarray(words), np.ascontiguousarray(byte.astype(np.uint8).reshape(n // 512, 16, m))


K, T, S, N, H, U = 512, 2048, 512, 512, 512, 1024


def setup_inputs():
    n = np.random.standard_normal
    s = mx_kscale(K)[:, None]
    u = mx_kscale(H)
    packed_xT = pack_weight(n((K, T)) * s)
    packed_w1 = pack_weight(n((K, H)) / np.sqrt(K) / s)
    packed_w2 = pack_weight(n((K, H)) / np.sqrt(K) / s)
    packed_w3 = pack_weight(n((H, N)) / np.sqrt(H) / u[:, None])
    return {
        "x_words": packed_xT[0],
        "x_scales": packed_xT[1],
        "w1_words": packed_w1[0],
        "w1_scales": packed_w1[1],
        "w2_words": packed_w2[0],
        "w2_scales": packed_w2[1],
        "gn": (np.random.uniform(0.5, 1.5, (H, 1)) * u[:, None]).astype(np.float32),
        "w3_words": packed_w3[0],
        "w3_scales": packed_w3[1],
        "mem": n((N, U)).astype(np.float32),
        "offs": striped(np.random.permutation(T)[:S]),
        "two": striped(np.random.permutation(T)[:S]),
        "n1": striped8(np.stack([np.random.permutation(S) for _ in range(8)])),
        "n2": striped8(np.stack([np.random.permutation(S) for _ in range(8)])),
        "n3": striped8(np.stack([np.random.permutation(S) for _ in range(8)])),
        "n4": striped8(np.stack([np.random.permutation(U)[:S] for _ in range(8)])),
    }


def reference(x_words, x_scales, w1_words, w1_scales, w2_words, w2_scales, gn, w3_words, w3_scales, mem, offs, two, n1, n2, n3, n4):
    old = f64(mem)[np.arange(N)[:, None], runs(n4, N)]
    x_two = unpack_weight(x_words, x_scales)[:, unstriped(two)]
    d = unpack_weight(w2_words, w2_scales).T @ x_two
    xq = unpack_weight(x_words, x_scales)[:, unstriped(offs)]
    y = unpack_weight(w1_words, w1_scales).T @ xq
    z = f64(gn) * (d * (y[np.arange(H)[:, None], runs(n1, H)] - y) + 0.5 * ((d[np.arange(H)[:, None], runs(n3, H)]) * (y[np.arange(H)[:, None], runs(n2, H)] - y)))
    h = unpack_weight(w3_words, w3_scales).T @ mxq(z, 0, "e4m3")
    nw = old + sigmoid(h) * (h - old)
    out = f64(mem).copy()
    out[np.arange(N)[:, None], runs(n4, N)] = nw
    return (out,) + planes(out)

@@ -1,0 +1,257 @@
+from contextlib import ExitStack
+
+import concourse.mybir as mybir
+
+F32 = mybir.dt.float32
+BF16 = mybir.dt.bfloat16
+I32 = mybir.dt.int32
+U32 = mybir.dt.uint32
+U16 = mybir.dt.uint16
+U8 = mybir.dt.uint8
+FP8X4 = mybir.dt.float8_e4m3fn_x4
+ALU = mybir.AluOpType
+ACT = mybir.ActivationFunctionType
+
+P = 128
+PACK = 4
+T = 2048
+S = 512
+F = 512
+U = 1024
+HALF = S // 2
+FLOPS = 3 * 2 * 512 * 512 * 512
+VEC_COLS = 640
+
+
+def tile_picked_twlflowbpaget_none_po_kernel(
+    tc, x_words, x_scales, w1_words, w1_scales, w2_words, w2_scales, gn, w3_words, w3_scales,
+    mem, offs, two, n1, n2, n3, n4, out_0, out_1, out_2,
+):
+    nc = tc.nc
+    with ExitStack() as ctx:
+        sb = ctx.enter_context(tc.tile_pool(name="sb", bufs=1))
+        ps = ctx.enter_context(tc.psum_pool(name="ps", bufs=8))
+
+        def words_of(ap):
+            return ap[0].rearrange("p n t -> p (n t)").bitcast(I32)
+
+        def load_list(ap, name):
+            tile = sb.tile([P, S // 16], U16, name=name)
+            nc.sync.dma_start(tile[:], ap)
+            return tile
+
+        def load_scale_rows(queue, tile, first, ap):
+            for q in range(4):
+                queue.dma_start(
+                    tile[32 * q + first : 32 * q + first + 4, :].bitcast(I32),
+                    ap[0, 4 * q : 4 * q + 4, :].bitcast(I32),
+                )
+
+        def load_weight_words(ap, name):
+            tile = sb.tile([P, F], I32, name=name)
+            nc.sync.dma_start(tile[:], words_of(ap))
+            return tile
+
+        def deal_words(raw, name):
+            tile = sb.tile([P, F], I32, name=name, align_bytes=64)
+            nc.vector.tensor_copy(
+                tile[:].rearrange("p (t a i) -> p a t i", t=PACK, i=4),
+                raw[:].rearrange("p (a i t) -> p a t i", t=PACK, i=4),
+            )
+            return tile
+
+        def deal_scales(raw, name):
+            tile = sb.tile([P, F], U8, name=name, align_bytes=64)
+            nc.vector.tensor_copy(
+                tile[:].rearrange("p (t m) -> p t m", t=PACK),
+                raw[:].rearrange("p (m t) -> p t m", t=PACK),
+            )
+            return tile
+
+        x_sc = sb.tile([P, T], U8, name="x_sc")
+        w_sc_raw = sb.tile([P, F], U8, name="w_sc_raw")
+        warm = sb.tile([P, 1], F32, name="warm")
+        warm_out = sb.tile([P, 1], F32, name="warm_out")
+        nc.vector.memset(x_sc[:].bitcast(I32), 0)
+        nc.vector.memset(w_sc_raw[:].bitcast(I32), 0)
+        w3_sc_raw = sb.tile([P, F], U8, name="w3_sc_raw")
+        nc.vector.memset(warm[:], 0.0)
+        nc.vector.memset(w3_sc_raw[:].bitcast(I32), 0)
+        nc.scalar.activation(warm_out[:], warm[:], ACT.Silu)
+
+        x_w = sb.tile([P, T], U32, name="x_w")
+        nc.sync.dma_start(x_w[:].bitcast(I32), words_of(x_words))
+        load_scale_rows(nc.sync, x_sc, 0, x_scales)
+        l_offs = load_list(offs, "l_offs")
+        w1_raw = load_weight_words(w1_words, "w1_raw")
+        l_two = load_list(two, "l_two")
+        load_scale_rows(nc.sync, w_sc_raw, 0, w1_scales)
+        load_scale_rows(nc.sync, w_sc_raw, 4, w2_scales)
+        w2_raw = load_weight_words(w2_words, "w2_raw")
+        l_n1 = load_list(n1, "l_n1")
+        l_n2 = load_list(n2, "l_n2")
+        gain = sb.tile([P, PACK], F32, name="gain")
+        nc.sync.dma_start(gain[:], gn.rearrange("(p t) o -> p (t o)", t=PACK))
+        l_n3 = load_list(n3, "l_n3")
+        w3_raw = load_weight_words(w3_words, "w3_raw")
+        l_n4 = load_list(n4, "l_n4")
+        mem_rows = mem.rearrange("(p t) u -> p t u", t=PACK)
+        out_rows = out_0.rearrange("(p t) u -> p t u", t=PACK)
+        page = []
+        for t in range(PACK):
+            tile = sb.tile([P, U], F32, name=f"page{t}")
+            nc.sync.dma_start(tile[:], mem_rows[:, t, :])
+            page.append(tile)
+            if t == 0:
+                load_scale_rows(nc.sync, w3_sc_raw, 0, w3_scales)
+
+        def pick_tokens(lst, name):
+            codes = sb.tile([P, S], U32, name=name + "_codes", align_bytes=64)
+            scales = sb.tile([P, S], U8, name=name + "_scales", align_bytes=64)
+            nc.vector.tensor_copy(codes[:], x_w[:].indirect(lst[:]))
+            nc.vector.tensor_copy(scales[:], x_sc[:].indirect(lst[:]))
+            return codes, scales
+
+        def project(out, w, w_sc, first, t, codes, scales):
+            cols = slice(P * t, P * (t + 1))
+            nc.tensor.matmul_mx(
+                out, lhsT=w[:, cols].bitcast(FP8X4), lhsT_scale=w_sc[first:P, cols],
+                rhs=codes.bitcast(FP8X4), rhs_scale=scales, start=True, stop=True,
+            )
+
+        xy_codes, xy_scales = pick_tokens(l_offs, "xy")
+        w1 = deal_words(w1_raw, "w1")
+        w_sc = deal_scales(w_sc_raw, "w_sc")
+        xd_codes, xd_scales = pick_tokens(l_two, "xd")
+        w2 = deal_words(w2_raw, "w2")
+
+        y_win = [sb.tile([P, S], F32, name=f"y_win{t}") for t in range(PACK)]
+        y_own = sb.tile([P, PACK, S], F32, name="y_own")
+        for t in range(PACK):
+            acc = ps.tile([P, S], F32, name="acc")
+            project(acc[:], w1, w_sc, 0, t, xy_codes[:], xy_scales[:])
+            nc.scalar.copy(y_win[t][:], acc[:])
+            nc.scalar.copy(y_own[:, t, :], acc[:])
+
+        half_gain = sb.tile([P, PACK], F32, name="half_gain")
+        nc.scalar.activation(half_gain[:], gain[:], ACT.Copy, scale=0.5)
+        d_win = [sb.tile([P, S], F32, name=f"d_win{t}") for t in range(PACK)]
+        d_own = sb.tile([P, PACK, S], F32, name="d_own")
+        d_acc = []
+        for t in range(PACK):
+            acc = ps.tile([P, S], F32, name="acc")
+            project(acc[:], w2, w_sc, 4, t, xd_codes[:], xd_scales[:])
+            nc.scalar.activation(d_win[t][:], acc[:], ACT.Copy, scale=half_gain[:, t : t + 1])
+            d_acc.append(acc)
+        for t in range(PACK):
+            nc.scalar.activation(d_own[:, t, :], d_acc[t][:], ACT.Copy, scale=gain[:, t : t + 1])
+
+        def cols_of(c):
+            return slice(HALF * c, HALF * (c + 1))
+
+        def entries(lst, c):
+            return lst[:, HALF // 16 * c : HALF // 16 * (c + 1)]
+
+        dy1 = [sb.tile([P, PACK, HALF], F32, name=f"dy1_{c}") for c in range(2)]
+        dy2 = [sb.tile([P, PACK, HALF], F32, name=f"dy2_{c}") for c in range(2)]
+        near = [sb.tile([P, PACK, HALF], F32, name=f"near{c}") for c in range(2)]
+        far = [sb.tile([P, PACK, HALF], F32, name=f"far{c}") for c in range(2)]
+        z_bf = [sb.tile([P, HALF, PACK], BF16, name=f"z_bf{c}", align_bytes=64) for c in range(2)]
+        z_codes = [sb.tile([P, HALF], U32, name=f"z_codes{c}", align_bytes=64) for c in range(2)]
+        z_scales = [sb.tile([P, HALF], U8, name=f"z_scales{c}", align_bytes=64) for c in range(2)]
+        keep = [sb.tile([P, S], F32, name=f"keep{t}") for t in range(PACK)]
+        fresh = [sb.tile([P, S], F32, name=f"fresh{t}") for t in range(PACK)]
+        kept = [sb.tile([P, S], F32, name=f"kept{t}") for t in range(PACK)]
+        tanh_h = [sb.tile([P, S], F32, name=f"tanh_h{t}") for t in range(PACK)]
+
+        def differences(c, t):
+            own = y_own[:, t, cols_of(c)]
+            nc.vector.tensor_tensor(dy1[c][:, t, :], y_win[t][:].indirect(entries(l_n1, c)), own, ALU.subtract)
+            nc.vector.tensor_tensor(dy2[c][:, t, :], y_win[t][:].indirect(entries(l_n2, c)), own, ALU.subtract)
+
+        def far_term(c, t):
+            nc.vector.tensor_tensor(far[c][:, t, :], d_win[t][:].indirect(entries(l_n3, c)), dy2[c][:, t, :], ALU.mult)
+
+        def near_term(c):
+            nc.vector.tensor_tensor(near[c][:], dy1[c][:], d_own[:, :, cols_of(c)], ALU.mult)
+
+        def sum_terms(c):
+            nc.vector.tensor_tensor(
+                z_bf[c][:].rearrange("p (a i) t -> p a t i", i=2),
+                near[c][:].rearrange("p t (a i) -> p a t i", i=2),
+                far[c][:].rearrange("p t (a i) -> p a t i", i=2),
+                ALU.add,
+            )
+
+        def last_layer(c):
+            nc.vector.quantize_mx(
+                out=z_codes[c][:].bitcast(FP8X4), scales=z_scales[c][:],
+                in_=z_bf[c][:].rearrange("p j t -> p (j t)"),
+            )
+            cols = cols_of(c)
+            for t in range(PACK):
+                acc = ps.tile([P, S], F32, name="acc")
+                h = acc[:, 0:HALF]
+                project(h, w3, w3_sc, 0, t, z_codes[c][:], z_scales[c][:])
+                nc.scalar.activation(tanh_h[t][:, cols], h, ACT.Tanh, scale=0.5)
+                nc.scalar.activation(keep[t][:, cols], tanh_h[t][:, cols], ACT.Copy, scale=-0.5, bias=0.5)
+                nc.scalar.activation(fresh[t][:, cols], h, ACT.Silu)
+
+        def old_part(c, t):
+            cols = cols_of(c)
+            nc.vector.tensor_tensor(kept[t][:, cols], page[t][:].indirect(entries(l_n4, c)), keep[t][:, cols], ALU.mult)
+
+        for t in range(PACK):
+            differences(0, t)
+        w3 = deal_words(w3_raw, "w3")
+        w3_sc = deal_scales(w3_sc_raw, "w3_sc")
+        differences(1, 0)
+        differences(1, 1)
+        for t in range(PACK):
+            far_term(0, t)
+        near_term(0)
+        differences(1, 2)
+        sum_terms(0)
+        differences(1, 3)
+        last_layer(0)
+        near_term(1)
+        for t in range(PACK):
+            far_term(1, t)
+        old_part(0, 0)
+        sum_terms(1)
+        old_part(0, 1)
+        last_layer(1)
+        old_part(0, 2)
+        old_part(0, 3)
+
+        out_bf = sb.tile([P, U, PACK], BF16, name="out_bf", align_bytes=64)
+        old_part(1, 0)
+        for t in range(PACK):
+            if t + 1 < PACK:
+                old_part(1, t + 1)
+            nc.vector.tensor_tensor(page[t][:].indirect(l_n4[:]), kept[t][:], fresh[t][:], ALU.add)
+            nc.sync.dma_start(out_rows[:, t, :], page[t][:])
+            if t < 2:
+                nc.scalar.copy(out_bf[:, :, t], page[t][:])
+            if t == 2:
+                nc.scalar.copy(out_bf[:, :, 2:4], page[t][:].unsqueeze(2).to_broadcast([P, U, 2]))
+        last = PACK - 1
+        nc.scalar.copy(out_bf[:, VEC_COLS:U, last], page[last][:, VEC_COLS:U])
+        nc.vector.tensor_copy(out_bf[:, 0 : U // 2, last], page[last][:, 0 : U // 2])
+        nc.vector.tensor_copy(out_bf[:, U // 2 : VEC_COLS, last], page[last][:, U // 2 : VEC_COLS])
+
+        out_codes = sb.tile([P, U], U32, name="out_codes", align_bytes=64)
+        out_scales = sb.tile([P, U], U8, name="out_scales", align_bytes=64)
+        out_words = words_of(out_1)
+        for c in range(2):
+            cols = slice(U // 2 * c, U // 2 * (c + 1))
+            nc.vector.quantize_mx(
+                out=out_codes[:, cols].bitcast(FP8X4), scales=out_scales[:, cols],
+                in_=out_bf[:, cols, :].rearrange("p u t -> p (u t)"),
+            )
+            nc.sync.dma_start(out_words[:, cols], out_codes[:, cols].bitcast(I32))
+        for q in range(4):
+            nc.sync.dma_start(
+                out_2[0, 4 * q : 4 * q + 4, :].bitcast(I32),
+                out_scales[32 * q : 32 * q + 4, :].bitcast(I32),
+            )

@@ -69,26 +69,29 @@ def tile_picked_twlflowbpaget_none_po_kernel(
             return tile
 
         x_sc = sb.tile([P, T], U8, name="x_sc")
-        w_sc_raw = sb.tile([P, F], U8, name="w_sc_raw")
+        w1_sc_raw = sb.tile([P, F], U8, name="w1_sc_raw", tag="after_w1", align_bytes=64)
+        w23_sc_raw = sb.tile([P, F], U8, name="w23_sc_raw")
         warm = sb.tile([P, 1], F32, name="warm")
-        warm_out = sb.tile([P, 1], F32, name="warm_out")
-        nc.vector.memset(x_sc[:].bitcast(I32), 0)
-        nc.vector.memset(w_sc_raw[:].bitcast(I32), 0)
-        w3_sc_raw = sb.tile([P, F], U8, name="w3_sc_raw")
+        nc.vector.memset(x_sc[:, 0 : T // 2].bitcast(I32), 0)
+        nc.gpsimd.memset(x_sc[:, T // 2 : T].bitcast(I32), 0)
+        nc.vector.memset(w1_sc_raw[:].bitcast(I32), 0)
+        nc.vector.memset(w23_sc_raw[:].bitcast(I32), 0)
         nc.vector.memset(warm[:], 0.0)
-        nc.vector.memset(w3_sc_raw[:].bitcast(I32), 0)
-        nc.scalar.activation(warm_out[:], warm[:], ACT.Silu)
 
+        l_offs = load_list(offs, "l_offs")
+        l_two = load_list(two, "l_two")
+        l_n1 = load_list(n1, "l_n1")
+        load_scale_rows(nc.sync, x_sc, 0, x_scales)
         x_w = sb.tile([P, T], U32, name="x_w")
         nc.sync.dma_start(x_w[:].bitcast(I32), words_of(x_words))
-        load_scale_rows(nc.sync, x_sc, 0, x_scales)
-        l_offs = load_list(offs, "l_offs")
+        load_scale_rows(nc.sync, w1_sc_raw, 0, w1_scales)
+        y_win = [sb.tile([P, 2 * S], F32, name=f"y_win{t}") for t in range(PACK)]
+        for t in range(PACK):
+            nc.scalar.activation(y_win[t][:, S : 2 * S], warm[:].to_broadcast([P, S]), ACT.Silu)
         w1_raw = load_weight_words(w1_words, "w1_raw")
-        l_two = load_list(two, "l_two")
-        load_scale_rows(nc.sync, w_sc_raw, 0, w1_scales)
-        load_scale_rows(nc.sync, w_sc_raw, 4, w2_scales)
         w2_raw = load_weight_words(w2_words, "w2_raw")
-        l_n1 = load_list(n1, "l_n1")
+        load_scale_rows(nc.sync, w23_sc_raw, 0, w2_scales)
+        load_scale_rows(nc.sync, w23_sc_raw, 4, w3_scales)
         l_n2 = load_list(n2, "l_n2")
         gain = sb.tile([P, PACK], F32, name="gain")
         nc.sync.dma_start(gain[:], gn.rearrange("(p t) o -> p (t o)", t=PACK))
@@ -102,15 +105,16 @@ def tile_picked_twlflowbpaget_none_po_kernel(
             tile = sb.tile([P, U], F32, name=f"page{t}")
             nc.sync.dma_start(tile[:], mem_rows[:, t, :])
             page.append(tile)
-            if t == 0:
-                load_scale_rows(nc.sync, w3_sc_raw, 0, w3_scales)
 
-        def pick_tokens(lst, name):
-            codes = sb.tile([P, S], U32, name=name + "_codes", align_bytes=64)
-            scales = sb.tile([P, S], U8, name=name + "_scales", align_bytes=64)
-            nc.vector.tensor_copy(codes[:], x_w[:].indirect(lst[:]))
+        def pick_scales(lst, name):
+            scales = sb.tile([P, S], U8, name=name, align_bytes=64)
             nc.vector.tensor_copy(scales[:], x_sc[:].indirect(lst[:]))
-            return codes, scales
+            return scales
+
+        def pick_codes(lst, name, tag):
+            codes = sb.tile([P, S], U32, name=name, tag=tag, align_bytes=64)
+            nc.vector.tensor_copy(codes[:], x_w[:].indirect(lst[:]))
+            return codes
 
         def project(out, w, w_sc, first, t, codes, scales):
             cols = slice(P * t, P * (t + 1))
@@ -119,18 +123,24 @@ def tile_picked_twlflowbpaget_none_po_kernel(
                 rhs=codes.bitcast(FP8X4), rhs_scale=scales, start=True, stop=True,
             )
 
-        xy_codes, xy_scales = pick_tokens(l_offs, "xy")
-        w1 = deal_words(w1_raw, "w1")
-        w_sc = deal_scales(w_sc_raw, "w_sc")
-        xd_codes, xd_scales = pick_tokens(l_two, "xd")
-        w2 = deal_words(w2_raw, "w2")
+        def cols_of(c):
+            return slice(HALF * c, HALF * (c + 1))
 
-        y_win = [sb.tile([P, S], F32, name=f"y_win{t}") for t in range(PACK)]
+        xy_scales = pick_scales(l_offs, "xy_scales")
+        xd_scales = pick_scales(l_two, "xd_scales")
+        xy_codes = pick_codes(l_offs, "xy_codes", "xy_codes")
+        w1 = deal_words(w1_raw, "w1")
+        w1_sc = deal_scales(w1_sc_raw, "w1_sc")
+        xd_codes = pick_codes(l_two, "xd_codes", "after_w1")
+        w2 = deal_words(w2_raw, "w2")
+        w23_sc = deal_scales(w23_sc_raw, "w23_sc")
+        w3 = deal_words(w3_raw, "w3")
+
         y_own = sb.tile([P, PACK, S], F32, name="y_own")
         for t in range(PACK):
             acc = ps.tile([P, S], F32, name="acc")
-            project(acc[:], w1, w_sc, 0, t, xy_codes[:], xy_scales[:])
-            nc.scalar.copy(y_win[t][:], acc[:])
+            project(acc[:], w1, w1_sc, 0, t, xy_codes[:], xy_scales[:])
+            nc.scalar.copy(y_win[t][:, 0:S], acc[:])
             nc.scalar.copy(y_own[:, t, :], acc[:])
 
         half_gain = sb.tile([P, PACK], F32, name="half_gain")
@@ -140,46 +150,41 @@ def tile_picked_twlflowbpaget_none_po_kernel(
         d_acc = []
         for t in range(PACK):
             acc = ps.tile([P, S], F32, name="acc")
-            project(acc[:], w2, w_sc, 4, t, xd_codes[:], xd_scales[:])
+            project(acc[:], w2, w23_sc, 0, t, xd_codes[:], xd_scales[:])
             nc.scalar.activation(d_win[t][:], acc[:], ACT.Copy, scale=half_gain[:, t : t + 1])
             d_acc.append(acc)
         for t in range(PACK):
             nc.scalar.activation(d_own[:, t, :], d_acc[t][:], ACT.Copy, scale=gain[:, t : t + 1])
 
-        def cols_of(c):
-            return slice(HALF * c, HALF * (c + 1))
-
         def entries(lst, c):
             return lst[:, HALF // 16 * c : HALF // 16 * (c + 1)]
 
-        dy1 = [sb.tile([P, PACK, HALF], F32, name=f"dy1_{c}") for c in range(2)]
-        dy2 = [sb.tile([P, PACK, HALF], F32, name=f"dy2_{c}") for c in range(2)]
-        near = [sb.tile([P, PACK, HALF], F32, name=f"near{c}") for c in range(2)]
-        far = [sb.tile([P, PACK, HALF], F32, name=f"far{c}") for c in range(2)]
-        z_bf = [sb.tile([P, HALF, PACK], BF16, name=f"z_bf{c}", align_bytes=64) for c in range(2)]
+        dy1 = sb.tile([P, PACK, S], F32, name="dy1")
+        dy2 = sb.tile([P, PACK, S], F32, name="dy2")
+        near = sb.tile([P, PACK, HALF], F32, name="near")
+        far = sb.tile([P, PACK, HALF], F32, name="far")
+        z_bf = [sb.tile([P, HALF, PACK], BF16, name=f"z_bf{c}", tag=f"z_bf{c}", align_bytes=64) for c in range(2)]
         z_codes = [sb.tile([P, HALF], U32, name=f"z_codes{c}", align_bytes=64) for c in range(2)]
         z_scales = [sb.tile([P, HALF], U8, name=f"z_scales{c}", align_bytes=64) for c in range(2)]
         keep = [sb.tile([P, S], F32, name=f"keep{t}") for t in range(PACK)]
         fresh = [sb.tile([P, S], F32, name=f"fresh{t}") for t in range(PACK)]
-        kept = [sb.tile([P, S], F32, name=f"kept{t}") for t in range(PACK)]
         tanh_h = [sb.tile([P, S], F32, name=f"tanh_h{t}") for t in range(PACK)]
 
-        def differences(c, t):
-            own = y_own[:, t, cols_of(c)]
-            nc.vector.tensor_tensor(dy1[c][:, t, :], y_win[t][:].indirect(entries(l_n1, c)), own, ALU.subtract)
-            nc.vector.tensor_tensor(dy2[c][:, t, :], y_win[t][:].indirect(entries(l_n2, c)), own, ALU.subtract)
+        def differences(t):
+            nc.vector.tensor_tensor(dy2[:, t, :], y_win[t][:].indirect(l_n2[:]), y_own[:, t, :], ALU.subtract)
+            nc.vector.tensor_tensor(dy1[:, t, :], y_win[t][:].indirect(l_n1[:]), y_own[:, t, :], ALU.subtract)
 
         def far_term(c, t):
-            nc.vector.tensor_tensor(far[c][:, t, :], d_win[t][:].indirect(entries(l_n3, c)), dy2[c][:, t, :], ALU.mult)
+            nc.vector.tensor_tensor(far[:, t, :], d_win[t][:].indirect(entries(l_n3, c)), dy2[:, t, cols_of(c)], ALU.mult)
 
         def near_term(c):
-            nc.vector.tensor_tensor(near[c][:], dy1[c][:], d_own[:, :, cols_of(c)], ALU.mult)
+            nc.vector.tensor_tensor(near[:], dy1[:, :, cols_of(c)], d_own[:, :, cols_of(c)], ALU.mult)
 
         def sum_terms(c):
             nc.vector.tensor_tensor(
                 z_bf[c][:].rearrange("p (a i) t -> p a t i", i=2),
-                near[c][:].rearrange("p t (a i) -> p a t i", i=2),
-                far[c][:].rearrange("p t (a i) -> p a t i", i=2),
+                near[:].rearrange("p t (a i) -> p a t i", i=2),
+                far[:].rearrange("p t (a i) -> p a t i", i=2),
                 ALU.add,
             )
 
@@ -189,47 +194,42 @@ def tile_picked_twlflowbpaget_none_po_kernel(
                 in_=z_bf[c][:].rearrange("p j t -> p (j t)"),
             )
             cols = cols_of(c)
+            hs = []
             for t in range(PACK):
                 acc = ps.tile([P, S], F32, name="acc")
                 h = acc[:, 0:HALF]
-                project(h, w3, w3_sc, 0, t, z_codes[c][:], z_scales[c][:])
+                hs.append(h)
+                project(h, w3, w23_sc, 4, t, z_codes[c][:], z_scales[c][:])
                 nc.scalar.activation(tanh_h[t][:, cols], h, ACT.Tanh, scale=0.5)
                 nc.scalar.activation(keep[t][:, cols], tanh_h[t][:, cols], ACT.Copy, scale=-0.5, bias=0.5)
-                nc.scalar.activation(fresh[t][:, cols], h, ACT.Silu)
+                if c == 1:
+                    nc.scalar.activation(fresh[t][:, cols], h, ACT.Silu)
+            if c == 0:
+                for t in range(PACK):
+                    nc.scalar.activation(fresh[t][:, cols], hs[t], ACT.Silu)
 
         def old_part(c, t):
             cols = cols_of(c)
-            nc.vector.tensor_tensor(kept[t][:, cols], page[t][:].indirect(entries(l_n4, c)), keep[t][:, cols], ALU.mult)
+            nc.vector.tensor_tensor(work[:, t, cols], page[t][:].indirect(entries(l_n4, c)), keep[t][:, cols], ALU.mult)
 
         for t in range(PACK):
-            differences(0, t)
-        w3 = deal_words(w3_raw, "w3")
-        w3_sc = deal_scales(w3_sc_raw, "w3_sc")
-        differences(1, 0)
-        differences(1, 1)
+            differences(t)
+        for c in range(2):
+            near_term(c)
+            for t in range(PACK):
+                far_term(c, t)
+            sum_terms(c)
+            last_layer(c)
+        work = sb.tile([P, PACK, S], F32, name="work", tag="z_bf1", align_bytes=64)
         for t in range(PACK):
-            far_term(0, t)
-        near_term(0)
-        differences(1, 2)
-        sum_terms(0)
-        differences(1, 3)
-        last_layer(0)
-        near_term(1)
-        for t in range(PACK):
-            far_term(1, t)
-        old_part(0, 0)
-        sum_terms(1)
-        old_part(0, 1)
-        last_layer(1)
-        old_part(0, 2)
-        old_part(0, 3)
+            old_part(0, t)
 
         out_bf = sb.tile([P, U, PACK], BF16, name="out_bf", align_bytes=64)
         old_part(1, 0)
         for t in range(PACK):
             if t + 1 < PACK:
                 old_part(1, t + 1)
-            nc.vector.tensor_tensor(page[t][:].indirect(l_n4[:]), kept[t][:], fresh[t][:], ALU.add)
+            nc.vector.tensor_tensor(page[t][:].indirect(l_n4[:]), work[:, t, :], fresh[t][:], ALU.add)
             nc.sync.dma_start(out_rows[:, t, :], page[t][:])
             if t < 2:
                 nc.scalar.copy(out_bf[:, :, t], page[t][:])

@@ -1,6 +1,7 @@
 from contextlib import ExitStack
 
 import concourse.mybir as mybir
+from concourse.masks import make_identity
 
 F32 = mybir.dt.float32
 BF16 = mybir.dt.bfloat16
@@ -70,7 +71,7 @@ def tile_picked_twlflowbpaget_none_po_kernel(
 
         x_sc = sb.tile([P, T], U8, name="x_sc")
         w1_sc_raw = sb.tile([P, F], U8, name="w1_sc_raw", tag="after_w1", align_bytes=64)
-        w23_sc_raw = sb.tile([P, F], U8, name="w23_sc_raw")
+        w23_sc_raw = sb.tile([P, F], U8, name="w23_sc_raw", tag="after_w23")
         warm = sb.tile([P, 1], F32, name="warm")
         nc.vector.memset(x_sc[:, 0 : T // 2].bitcast(I32), 0)
         nc.gpsimd.memset(x_sc[:, T // 2 : T].bitcast(I32), 0)
@@ -80,23 +81,25 @@ def tile_picked_twlflowbpaget_none_po_kernel(
 
         l_offs = load_list(offs, "l_offs")
         l_two = load_list(two, "l_two")
-        l_n1 = load_list(n1, "l_n1")
+        l_n2 = load_list(n2, "l_n2")
         load_scale_rows(nc.sync, x_sc, 0, x_scales)
         x_w = sb.tile([P, T], U32, name="x_w")
         nc.sync.dma_start(x_w[:].bitcast(I32), words_of(x_words))
-        load_scale_rows(nc.sync, w1_sc_raw, 0, w1_scales)
-        y_win = [sb.tile([P, 2 * S], F32, name=f"y_win{t}") for t in range(PACK)]
-        for t in range(PACK):
-            nc.scalar.activation(y_win[t][:, S : 2 * S], warm[:].to_broadcast([P, S]), ACT.Silu)
         w1_raw = load_weight_words(w1_words, "w1_raw")
-        w2_raw = load_weight_words(w2_words, "w2_raw")
+        load_scale_rows(nc.sync, w1_sc_raw, 0, w1_scales)
         load_scale_rows(nc.sync, w23_sc_raw, 0, w2_scales)
+        w2_raw = load_weight_words(w2_words, "w2_raw")
         load_scale_rows(nc.sync, w23_sc_raw, 4, w3_scales)
-        l_n2 = load_list(n2, "l_n2")
+        l_n1 = load_list(n1, "l_n1")
         gain = sb.tile([P, PACK], F32, name="gain")
         nc.sync.dma_start(gain[:], gn.rearrange("(p t) o -> p (t o)", t=PACK))
-        l_n3 = load_list(n3, "l_n3")
         w3_raw = load_weight_words(w3_words, "w3_raw")
+        l_n3 = load_list(n3, "l_n3")
+        y_win = [sb.tile([P, 2 * S], F32, name=f"y_win{t}") for t in range(PACK)]
+        for t in range(PACK):
+            nc.scalar.activation(y_win[t][:, S : 2 * S], warm[:].to_broadcast([P, S]), ACT.Sigmoid)
+        identity = sb.tile([P, P], F32, name="identity")
+        make_identity(nc, identity[:])
         l_n4 = load_list(n4, "l_n4")
         mem_rows = mem.rearrange("(p t) u -> p t u", t=PACK)
         out_rows = out_0.rearrange("(p t) u -> p t u", t=PACK)
@@ -151,62 +154,77 @@ def tile_picked_twlflowbpaget_none_po_kernel(
         for t in range(PACK):
             acc = ps.tile([P, S], F32, name="acc")
             project(acc[:], w2, w23_sc, 0, t, xd_codes[:], xd_scales[:])
-            nc.scalar.activation(d_win[t][:], acc[:], ACT.Copy, scale=half_gain[:, t : t + 1])
+            nc.scalar.activation(d_own[:, t, :], acc[:], ACT.Copy, scale=gain[:, t : t + 1])
             d_acc.append(acc)
         for t in range(PACK):
-            nc.scalar.activation(d_own[:, t, :], d_acc[t][:], ACT.Copy, scale=gain[:, t : t + 1])
+            nc.scalar.activation(d_win[t][:], d_acc[t][:], ACT.Copy, scale=half_gain[:, t : t + 1])
 
         def entries(lst, c):
             return lst[:, HALF // 16 * c : HALF // 16 * (c + 1)]
 
         dy1 = sb.tile([P, PACK, S], F32, name="dy1")
-        dy2 = sb.tile([P, PACK, S], F32, name="dy2")
-        near = sb.tile([P, PACK, HALF], F32, name="near")
-        far = sb.tile([P, PACK, HALF], F32, name="far")
-        z_bf = [sb.tile([P, HALF, PACK], BF16, name=f"z_bf{c}", tag=f"z_bf{c}", align_bytes=64) for c in range(2)]
+        dy2 = sb.tile([P, PACK, S], F32, name="dy2", tag="after_w23")
+        near_first = sb.tile([P, PACK, HALF], F32, name="near_first")
+        near = [near_first[:], dy2[:, :, cols_of(0)]]
+        far = [dy1[:, :, cols_of(c)] for c in range(2)]
+        z_bf = sb.tile([P, HALF, PACK], BF16, name="z_bf", tag="z_bf", align_bytes=64)
         z_codes = [sb.tile([P, HALF], U32, name=f"z_codes{c}", align_bytes=64) for c in range(2)]
         z_scales = [sb.tile([P, HALF], U8, name=f"z_scales{c}", align_bytes=64) for c in range(2)]
         keep = [sb.tile([P, S], F32, name=f"keep{t}") for t in range(PACK)]
         fresh = [sb.tile([P, S], F32, name=f"fresh{t}") for t in range(PACK)]
-        tanh_h = [sb.tile([P, S], F32, name=f"tanh_h{t}") for t in range(PACK)]
 
         def differences(t):
             nc.vector.tensor_tensor(dy2[:, t, :], y_win[t][:].indirect(l_n2[:]), y_own[:, t, :], ALU.subtract)
             nc.vector.tensor_tensor(dy1[:, t, :], y_win[t][:].indirect(l_n1[:]), y_own[:, t, :], ALU.subtract)
 
         def far_term(c, t):
-            nc.vector.tensor_tensor(far[:, t, :], d_win[t][:].indirect(entries(l_n3, c)), dy2[:, t, cols_of(c)], ALU.mult)
+            nc.vector.tensor_tensor(far[c][:, t, :], d_win[t][:].indirect(entries(l_n3, c)), dy2[:, t, cols_of(c)], ALU.mult)
 
         def near_term(c):
-            nc.vector.tensor_tensor(near[:], dy1[:, :, cols_of(c)], d_own[:, :, cols_of(c)], ALU.mult)
+            nc.vector.tensor_tensor(near[c], dy1[:, :, cols_of(c)], d_own[:, :, cols_of(c)], ALU.mult)
 
         def sum_terms(c):
             nc.vector.tensor_tensor(
-                z_bf[c][:].rearrange("p (a i) t -> p a t i", i=2),
-                near[:].rearrange("p t (a i) -> p a t i", i=2),
-                far[:].rearrange("p t (a i) -> p a t i", i=2),
+                z_bf[:].rearrange("p (a i) t -> p a t i", i=2),
+                near[c].rearrange("p t (a i) -> p a t i", i=2),
+                far[c].rearrange("p t (a i) -> p a t i", i=2),
                 ALU.add,
             )
 
-        def last_layer(c):
+        def sum_terms_turned(c):
+            blocks = range(HALF // P)
+            turned = [ps.tile([P, S], F32, name="acc") for b in blocks]
+            for t in range(PACK):
+                for b in blocks:
+                    for first, term in ((True, near[c]), (False, far[c])):
+                        nc.tensor.matmul(
+                            turned[b][:, P * t : P * (t + 1)], lhsT=term[:, t, P * b : P * (b + 1)], rhs=identity[:],
+                            is_transpose=True, start=first, stop=not first,
+                        )
+            z_words = z_bf[:].rearrange("p j t -> p (j t)").bitcast(F32).rearrange("p (j u) -> p j u", u=2)
+            for b in blocks:
+                rounded = sb.tile([P, F], BF16, name=f"rounded{b}")
+                nc.scalar.copy(
+                    rounded[:].rearrange("j (u p e) -> j u p e", u=2, e=2),
+                    turned[b][:].rearrange("j (u e p) -> j u p e", u=2, e=2),
+                )
+                back = ps.tile([P, S], F32, name="acc")
+                for u in range(2):
+                    nc.tensor.transpose(back[:, P * u : P * (u + 1)], rounded[:].bitcast(F32)[:, P * u : P * (u + 1)], identity[:])
+                nc.scalar.copy(
+                    z_words[:, P * b : P * (b + 1), :],
+                    back[:, 0 : 2 * P].rearrange("p (u j) -> p j u", u=2),
+                )
+
+        def last_layer(c, h):
             nc.vector.quantize_mx(
                 out=z_codes[c][:].bitcast(FP8X4), scales=z_scales[c][:],
-                in_=z_bf[c][:].rearrange("p j t -> p (j t)"),
+                in_=z_bf[:].rearrange("p j t -> p (j t)"),
             )
             cols = cols_of(c)
-            hs = []
             for t in range(PACK):
-                acc = ps.tile([P, S], F32, name="acc")
-                h = acc[:, 0:HALF]
-                hs.append(h)
-                project(h, w3, w23_sc, 4, t, z_codes[c][:], z_scales[c][:])
-                nc.scalar.activation(tanh_h[t][:, cols], h, ACT.Tanh, scale=0.5)
-                nc.scalar.activation(keep[t][:, cols], tanh_h[t][:, cols], ACT.Copy, scale=-0.5, bias=0.5)
-                if c == 1:
-                    nc.scalar.activation(fresh[t][:, cols], h, ACT.Silu)
-            if c == 0:
-                for t in range(PACK):
-                    nc.scalar.activation(fresh[t][:, cols], hs[t], ACT.Silu)
+                project(h[t][:, cols], w3, w23_sc, 4, t, z_codes[c][:], z_scales[c][:])
+                nc.scalar.activation(keep[t][:, cols], h[t][:, cols], ACT.Sigmoid, scale=-1.0)
 
         def old_part(c, t):
             cols = cols_of(c)
@@ -218,23 +236,31 @@ def tile_picked_twlflowbpaget_none_po_kernel(
             near_term(c)
             for t in range(PACK):
                 far_term(c, t)
-            sum_terms(c)
-            last_layer(c)
-        work = sb.tile([P, PACK, S], F32, name="work", tag="z_bf1", align_bytes=64)
+            if c == 0:
+                sum_terms_turned(c)
+                h = [ps.tile([P, S], F32, name="acc") for t in range(PACK)]
+            else:
+                sum_terms(c)
+            last_layer(c, h)
+        work = sb.tile([P, PACK, S], F32, name="work", tag="z_bf", align_bytes=64)
         for t in range(PACK):
-            old_part(0, t)
+            nc.scalar.activation(fresh[t][:], h[t][:], ACT.Silu)
+        for c in range(2):
+            for t in range(2):
+                old_part(c, t)
+        for t in range(2, PACK):
+            nc.vector.tensor_tensor(work[:, t, :], page[t][:].indirect(l_n4[:]), keep[t][:], ALU.mult)
 
         out_bf = sb.tile([P, U, PACK], BF16, name="out_bf", align_bytes=64)
-        old_part(1, 0)
         for t in range(PACK):
-            if t + 1 < PACK:
-                old_part(1, t + 1)
             nc.vector.tensor_tensor(page[t][:].indirect(l_n4[:]), work[:, t, :], fresh[t][:], ALU.add)
             nc.sync.dma_start(out_rows[:, t, :], page[t][:])
             if t < 2:
                 nc.scalar.copy(out_bf[:, :, t], page[t][:])
             if t == 2:
-                nc.scalar.copy(out_bf[:, :, 2:4], page[t][:].unsqueeze(2).to_broadcast([P, U, 2]))
+                for c in range(2):
+                    cols = slice(U // 2 * c, U // 2 * (c + 1))
+                    nc.scalar.copy(out_bf[:, cols, 2:4], page[t][:, cols].unsqueeze(2).to_broadcast([P, U // 2, 2]))
         last = PACK - 1
         nc.scalar.copy(out_bf[:, VEC_COLS:U, last], page[last][:, VEC_COLS:U])
         nc.vector.tensor_copy(out_bf[:, 0 : U // 2, last], page[last][:, 0 : U // 2])
@@ -251,7 +277,8 @@ def tile_picked_twlflowbpaget_none_po_kernel(
             )
             nc.sync.dma_start(out_words[:, cols], out_codes[:, cols].bitcast(I32))
         for q in range(4):
-            nc.sync.dma_start(
+            queue = nc.scalar if q < 3 else nc.sync
+            queue.dma_start(
                 out_2[0, 4 * q : 4 * q + 4, :].bitcast(I32),
                 out_scales[32 * q : 32 * q + 4, :].bitcast(I32),
             )

@@ -21,7 +21,8 @@ F = 512
 U = 1024
 HALF = S // 2
 FLOPS = 3 * 2 * 512 * 512 * 512
-VEC_COLS = 640
+VEC_COLS = 768
+ORDER = (2, 0, 1, 3)
 
 
 def tile_picked_twlflowbpaget_none_po_kernel(
@@ -79,14 +80,14 @@ def tile_picked_twlflowbpaget_none_po_kernel(
         nc.vector.memset(w23_sc_raw[:].bitcast(I32), 0)
         nc.vector.memset(warm[:], 0.0)
 
+        w1_raw = load_weight_words(w1_words, "w1_raw")
         l_offs = load_list(offs, "l_offs")
         l_two = load_list(two, "l_two")
-        l_n2 = load_list(n2, "l_n2")
         load_scale_rows(nc.sync, x_sc, 0, x_scales)
         x_w = sb.tile([P, T], U32, name="x_w")
         nc.sync.dma_start(x_w[:].bitcast(I32), words_of(x_words))
-        w1_raw = load_weight_words(w1_words, "w1_raw")
         load_scale_rows(nc.sync, w1_sc_raw, 0, w1_scales)
+        l_n2 = load_list(n2, "l_n2")
         load_scale_rows(nc.sync, w23_sc_raw, 0, w2_scales)
         w2_raw = load_weight_words(w2_words, "w2_raw")
         load_scale_rows(nc.sync, w23_sc_raw, 4, w3_scales)
@@ -129,10 +130,10 @@ def tile_picked_twlflowbpaget_none_po_kernel(
         def cols_of(c):
             return slice(HALF * c, HALF * (c + 1))
 
+        w1 = deal_words(w1_raw, "w1")
         xy_scales = pick_scales(l_offs, "xy_scales")
         xd_scales = pick_scales(l_two, "xd_scales")
         xy_codes = pick_codes(l_offs, "xy_codes", "xy_codes")
-        w1 = deal_words(w1_raw, "w1")
         w1_sc = deal_scales(w1_sc_raw, "w1_sc")
         xd_codes = pick_codes(l_two, "xd_codes", "after_w1")
         w2 = deal_words(w2_raw, "w2")
@@ -222,13 +223,13 @@ def tile_picked_twlflowbpaget_none_po_kernel(
                 in_=z_bf[:].rearrange("p j t -> p (j t)"),
             )
             cols = cols_of(c)
-            for t in range(PACK):
+            for t in ORDER:
                 project(h[t][:, cols], w3, w23_sc, 4, t, z_codes[c][:], z_scales[c][:])
                 nc.scalar.activation(keep[t][:, cols], h[t][:, cols], ACT.Sigmoid, scale=-1.0)
 
         def old_part(c, t):
             cols = cols_of(c)
-            nc.vector.tensor_tensor(work[:, t, cols], page[t][:].indirect(entries(l_n4, c)), keep[t][:, cols], ALU.mult)
+            nc.vector.tensor_tensor(kept[t][:, cols], page[t][:].indirect(entries(l_n4, c)), keep[t][:, cols], ALU.mult)
 
         for t in range(PACK):
             differences(t)
@@ -242,26 +243,31 @@ def tile_picked_twlflowbpaget_none_po_kernel(
             else:
                 sum_terms(c)
             last_layer(c, h)
-        work = sb.tile([P, PACK, S], F32, name="work", tag="z_bf", align_bytes=64)
-        for t in range(PACK):
+        first, second, third, last = ORDER
+        work = sb.tile([P, PACK * S - HALF], F32, name="work", tag="z_bf", align_bytes=64)
+        starts = {last: 0, first: HALF, second: HALF + S, third: HALF + 2 * S}
+        kept = [work[:, starts[t] : starts[t] + S] for t in range(PACK)]
+        for t in ORDER:
             nc.scalar.activation(fresh[t][:], h[t][:], ACT.Silu)
-        for c in range(2):
-            for t in range(2):
-                old_part(c, t)
-        for t in range(2, PACK):
-            nc.vector.tensor_tensor(work[:, t, :], page[t][:].indirect(l_n4[:]), keep[t][:], ALU.mult)
+        for t in (first, second, last):
+            old_part(0, t)
+        for t in (first, second):
+            old_part(1, t)
+        nc.vector.tensor_tensor(kept[third], page[third][:].indirect(l_n4[:]), keep[third][:], ALU.mult)
 
         out_bf = sb.tile([P, U, PACK], BF16, name="out_bf", align_bytes=64)
-        for t in range(PACK):
-            nc.vector.tensor_tensor(page[t][:].indirect(l_n4[:]), work[:, t, :], fresh[t][:], ALU.add)
+        for t in ORDER:
+            nc.vector.tensor_tensor(page[t][:].indirect(l_n4[:]), kept[t], fresh[t][:], ALU.add)
             nc.sync.dma_start(out_rows[:, t, :], page[t][:])
-            if t < 2:
+            if t == first:
+                old_part(1, last)
+                nc.scalar.copy(out_bf[:, :, 2:4], page[t][:].unsqueeze(2).to_broadcast([P, U, 2]))
+            if t == second:
                 nc.scalar.copy(out_bf[:, :, t], page[t][:])
-            if t == 2:
+            if t == third:
                 for c in range(2):
                     cols = slice(U // 2 * c, U // 2 * (c + 1))
-                    nc.scalar.copy(out_bf[:, cols, 2:4], page[t][:, cols].unsqueeze(2).to_broadcast([P, U // 2, 2]))
-        last = PACK - 1
+                    nc.scalar.copy(out_bf[:, cols, t], page[t][:, cols])
         nc.scalar.copy(out_bf[:, VEC_COLS:U, last], page[last][:, VEC_COLS:U])
         nc.vector.tensor_copy(out_bf[:, 0 : U // 2, last], page[last][:, 0 : U // 2])
         nc.vector.tensor_copy(out_bf[:, U // 2 : VEC_COLS, last], page[last][:, U // 2 : VEC_COLS])
@@ -269,8 +275,7 @@ def tile_picked_twlflowbpaget_none_po_kernel(
         out_codes = sb.tile([P, U], U32, name="out_codes", align_bytes=64)
         out_scales = sb.tile([P, U], U8, name="out_scales", align_bytes=64)
         out_words = words_of(out_1)
-        for c in range(2):
-            cols = slice(U // 2 * c, U // 2 * (c + 1))
+        for cols in (slice(0, U // 2), slice(U // 2, VEC_COLS), slice(VEC_COLS, U)):
             nc.vector.quantize_mx(
                 out=out_codes[:, cols].bitcast(FP8X4), scales=out_scales[:, cols],
                 in_=out_bf[:, cols, :].rearrange("p u t -> p (u t)"),

from contextlib import ExitStack

import concourse.mybir as mybir
from concourse.masks import make_identity

F32 = mybir.dt.float32
BF16 = mybir.dt.bfloat16
I32 = mybir.dt.int32
U32 = mybir.dt.uint32
U16 = mybir.dt.uint16
U8 = mybir.dt.uint8
FP8X4 = mybir.dt.float8_e4m3fn_x4
ALU = mybir.AluOpType
ACT = mybir.ActivationFunctionType

P = 128
PACK = 4
T = 2048
S = 512
F = 512
U = 1024
HALF = S // 2
FLOPS = 3 * 2 * 512 * 512 * 512
VEC_COLS = 768
ORDER = (2, 0, 1, 3)


def tile_picked_twlflowbpaget_none_po_kernel(
    tc, x_words, x_scales, w1_words, w1_scales, w2_words, w2_scales, gn, w3_words, w3_scales,
    mem, offs, two, n1, n2, n3, n4, out_0, out_1, out_2,
):
    nc = tc.nc
    with ExitStack() as ctx:
        sb = ctx.enter_context(tc.tile_pool(name="sb", bufs=1))
        ps = ctx.enter_context(tc.psum_pool(name="ps", bufs=8))

        def words_of(ap):
            return ap[0].rearrange("p n t -> p (n t)").bitcast(I32)

        def load_list(ap, name):
            tile = sb.tile([P, S // 16], U16, name=name)
            nc.sync.dma_start(tile[:], ap)
            return tile

        def load_scale_rows(queue, tile, first, ap):
            for q in range(4):
                queue.dma_start(
                    tile[32 * q + first : 32 * q + first + 4, :].bitcast(I32),
                    ap[0, 4 * q : 4 * q + 4, :].bitcast(I32),
                )

        def load_weight_words(ap, name):
            tile = sb.tile([P, F], I32, name=name)
            nc.sync.dma_start(tile[:], words_of(ap))
            return tile

        def deal_words(raw, name):
            tile = sb.tile([P, F], I32, name=name, align_bytes=64)
            nc.vector.tensor_copy(
                tile[:].rearrange("p (t a i) -> p a t i", t=PACK, i=4),
                raw[:].rearrange("p (a i t) -> p a t i", t=PACK, i=4),
            )
            return tile

        def deal_scales(raw, name):
            tile = sb.tile([P, F], U8, name=name, align_bytes=64)
            nc.vector.tensor_copy(
                tile[:].rearrange("p (t m) -> p t m", t=PACK),
                raw[:].rearrange("p (m t) -> p t m", t=PACK),
            )
            return tile

        x_sc = sb.tile([P, T], U8, name="x_sc")
        w1_sc_raw = sb.tile([P, F], U8, name="w1_sc_raw", tag="after_w1", align_bytes=64)
        w23_sc_raw = sb.tile([P, F], U8, name="w23_sc_raw", tag="after_w23")
        warm = sb.tile([P, 1], F32, name="warm")
        nc.vector.memset(x_sc[:, 0 : T // 2].bitcast(I32), 0)
        nc.gpsimd.memset(x_sc[:, T // 2 : T].bitcast(I32), 0)
        nc.vector.memset(w1_sc_raw[:].bitcast(I32), 0)
        nc.vector.memset(w23_sc_raw[:].bitcast(I32), 0)
        nc.vector.memset(warm[:], 0.0)

        w1_raw = load_weight_words(w1_words, "w1_raw")
        l_offs = load_list(offs, "l_offs")
        l_two = load_list(two, "l_two")
        load_scale_rows(nc.sync, x_sc, 0, x_scales)
        x_w = sb.tile([P, T], U32, name="x_w")
        nc.sync.dma_start(x_w[:].bitcast(I32), words_of(x_words))
        load_scale_rows(nc.sync, w1_sc_raw, 0, w1_scales)
        l_n2 = load_list(n2, "l_n2")
        load_scale_rows(nc.sync, w23_sc_raw, 0, w2_scales)
        w2_raw = load_weight_words(w2_words, "w2_raw")
        load_scale_rows(nc.sync, w23_sc_raw, 4, w3_scales)
        l_n1 = load_list(n1, "l_n1")
        gain = sb.tile([P, PACK], F32, name="gain")
        nc.sync.dma_start(gain[:], gn.rearrange("(p t) o -> p (t o)", t=PACK))
        w3_raw = load_weight_words(w3_words, "w3_raw")
        l_n3 = load_list(n3, "l_n3")
        y_win = [sb.tile([P, 2 * S], F32, name=f"y_win{t}") for t in range(PACK)]
        for t in range(PACK):
            nc.scalar.activation(y_win[t][:, S : 2 * S], warm[:].to_broadcast([P, S]), ACT.Sigmoid)
        identity = sb.tile([P, P], F32, name="identity")
        make_identity(nc, identity[:])
        l_n4 = load_list(n4, "l_n4")
        mem_rows = mem.rearrange("(p t) u -> p t u", t=PACK)
        out_rows = out_0.rearrange("(p t) u -> p t u", t=PACK)
        page = []
        for t in range(PACK):
            tile = sb.tile([P, U], F32, name=f"page{t}")
            nc.sync.dma_start(tile[:], mem_rows[:, t, :])
            page.append(tile)

        def pick_scales(lst, name):
            scales = sb.tile([P, S], U8, name=name, align_bytes=64)
            nc.vector.tensor_copy(scales[:], x_sc[:].indirect(lst[:]))
            return scales

        def pick_codes(lst, name, tag):
            codes = sb.tile([P, S], U32, name=name, tag=tag, align_bytes=64)
            nc.vector.tensor_copy(codes[:], x_w[:].indirect(lst[:]))
            return codes

        def project(out, w, w_sc, first, t, codes, scales):
            cols = slice(P * t, P * (t + 1))
            nc.tensor.matmul_mx(
                out, lhsT=w[:, cols].bitcast(FP8X4), lhsT_scale=w_sc[first:P, cols],
                rhs=codes.bitcast(FP8X4), rhs_scale=scales, start=True, stop=True,
            )

        def cols_of(c):
            return slice(HALF * c, HALF * (c + 1))

        w1 = deal_words(w1_raw, "w1")
        xy_scales = pick_scales(l_offs, "xy_scales")
        xd_scales = pick_scales(l_two, "xd_scales")
        xy_codes = pick_codes(l_offs, "xy_codes", "xy_codes")
        w1_sc = deal_scales(w1_sc_raw, "w1_sc")
        xd_codes = pick_codes(l_two, "xd_codes", "after_w1")
        w2 = deal_words(w2_raw, "w2")
        w23_sc = deal_scales(w23_sc_raw, "w23_sc")
        w3 = deal_words(w3_raw, "w3")

        y_own = sb.tile([P, PACK, S], F32, name="y_own")
        for t in range(PACK):
            acc = ps.tile([P, S], F32, name="acc")
            project(acc[:], w1, w1_sc, 0, t, xy_codes[:], xy_scales[:])
            nc.scalar.copy(y_win[t][:, 0:S], acc[:])
            nc.scalar.copy(y_own[:, t, :], acc[:])

        half_gain = sb.tile([P, PACK], F32, name="half_gain")
        nc.scalar.activation(half_gain[:], gain[:], ACT.Copy, scale=0.5)
        d_win = [sb.tile([P, S], F32, name=f"d_win{t}") for t in range(PACK)]
        d_own = sb.tile([P, PACK, S], F32, name="d_own")
        d_acc = []
        for t in range(PACK):
            acc = ps.tile([P, S], F32, name="acc")
            project(acc[:], w2, w23_sc, 0, t, xd_codes[:], xd_scales[:])
            nc.scalar.activation(d_own[:, t, :], acc[:], ACT.Copy, scale=gain[:, t : t + 1])
            d_acc.append(acc)
        for t in range(PACK):
            nc.scalar.activation(d_win[t][:], d_acc[t][:], ACT.Copy, scale=half_gain[:, t : t + 1])

        def entries(lst, c):
            return lst[:, HALF // 16 * c : HALF // 16 * (c + 1)]

        dy1 = sb.tile([P, PACK, S], F32, name="dy1")
        dy2 = sb.tile([P, PACK, S], F32, name="dy2", tag="after_w23")
        near_first = sb.tile([P, PACK, HALF], F32, name="near_first")
        near = [near_first[:], dy2[:, :, cols_of(0)]]
        far = [dy1[:, :, cols_of(c)] for c in range(2)]
        z_bf = sb.tile([P, HALF, PACK], BF16, name="z_bf", tag="z_bf", align_bytes=64)
        z_codes = [sb.tile([P, HALF], U32, name=f"z_codes{c}", align_bytes=64) for c in range(2)]
        z_scales = [sb.tile([P, HALF], U8, name=f"z_scales{c}", align_bytes=64) for c in range(2)]
        keep = [sb.tile([P, S], F32, name=f"keep{t}") for t in range(PACK)]
        fresh = [sb.tile([P, S], F32, name=f"fresh{t}") for t in range(PACK)]

        def differences(t):
            nc.vector.tensor_tensor(dy2[:, t, :], y_win[t][:].indirect(l_n2[:]), y_own[:, t, :], ALU.subtract)
            nc.vector.tensor_tensor(dy1[:, t, :], y_win[t][:].indirect(l_n1[:]), y_own[:, t, :], ALU.subtract)

        def far_term(c, t):
            nc.vector.tensor_tensor(far[c][:, t, :], d_win[t][:].indirect(entries(l_n3, c)), dy2[:, t, cols_of(c)], ALU.mult)

        def near_term(c):
            nc.vector.tensor_tensor(near[c], dy1[:, :, cols_of(c)], d_own[:, :, cols_of(c)], ALU.mult)

        def sum_terms(c):
            nc.vector.tensor_tensor(
                z_bf[:].rearrange("p (a i) t -> p a t i", i=2),
                near[c].rearrange("p t (a i) -> p a t i", i=2),
                far[c].rearrange("p t (a i) -> p a t i", i=2),
                ALU.add,
            )

        def sum_terms_turned(c):
            blocks = range(HALF // P)
            turned = [ps.tile([P, S], F32, name="acc") for b in blocks]
            for t in range(PACK):
                for b in blocks:
                    for first, term in ((True, near[c]), (False, far[c])):
                        nc.tensor.matmul(
                            turned[b][:, P * t : P * (t + 1)], lhsT=term[:, t, P * b : P * (b + 1)], rhs=identity[:],
                            is_transpose=True, start=first, stop=not first,
                        )
            z_words = z_bf[:].rearrange("p j t -> p (j t)").bitcast(F32).rearrange("p (j u) -> p j u", u=2)
            for b in blocks:
                rounded = sb.tile([P, F], BF16, name=f"rounded{b}")
                nc.scalar.copy(
                    rounded[:].rearrange("j (u p e) -> j u p e", u=2, e=2),
                    turned[b][:].rearrange("j (u e p) -> j u p e", u=2, e=2),
                )
                back = ps.tile([P, S], F32, name="acc")
                for u in range(2):
                    nc.tensor.transpose(back[:, P * u : P * (u + 1)], rounded[:].bitcast(F32)[:, P * u : P * (u + 1)], identity[:])
                nc.scalar.copy(
                    z_words[:, P * b : P * (b + 1), :],
                    back[:, 0 : 2 * P].rearrange("p (u j) -> p j u", u=2),
                )

        def last_layer(c, h):
            nc.vector.quantize_mx(
                out=z_codes[c][:].bitcast(FP8X4), scales=z_scales[c][:],
                in_=z_bf[:].rearrange("p j t -> p (j t)"),
            )
            cols = cols_of(c)
            for t in ORDER:
                project(h[t][:, cols], w3, w23_sc, 4, t, z_codes[c][:], z_scales[c][:])
                nc.scalar.activation(keep[t][:, cols], h[t][:, cols], ACT.Sigmoid, scale=-1.0)

        def old_part(c, t):
            cols = cols_of(c)
            nc.vector.tensor_tensor(kept[t][:, cols], page[t][:].indirect(entries(l_n4, c)), keep[t][:, cols], ALU.mult)

        for t in range(PACK):
            differences(t)
        for c in range(2):
            near_term(c)
            for t in range(PACK):
                far_term(c, t)
            if c == 0:
                sum_terms_turned(c)
                h = [ps.tile([P, S], F32, name="acc") for t in range(PACK)]
            else:
                sum_terms(c)
            last_layer(c, h)
        first, second, third, last = ORDER
        work = sb.tile([P, PACK * S - HALF], F32, name="work", tag="z_bf", align_bytes=64)
        starts = {last: 0, first: HALF, second: HALF + S, third: HALF + 2 * S}
        kept = [work[:, starts[t] : starts[t] + S] for t in range(PACK)]
        for t in ORDER:
            nc.scalar.activation(fresh[t][:], h[t][:], ACT.Silu)
        for t in (first, second, last):
            old_part(0, t)
        for t in (first, second):
            old_part(1, t)
        nc.vector.tensor_tensor(kept[third], page[third][:].indirect(l_n4[:]), keep[third][:], ALU.mult)

        out_bf = sb.tile([P, U, PACK], BF16, name="out_bf", align_bytes=64)
        for t in ORDER:
            nc.vector.tensor_tensor(page[t][:].indirect(l_n4[:]), kept[t], fresh[t][:], ALU.add)
            nc.sync.dma_start(out_rows[:, t, :], page[t][:])
            if t == first:
                old_part(1, last)
                nc.scalar.copy(out_bf[:, :, 2:4], page[t][:].unsqueeze(2).to_broadcast([P, U, 2]))
            if t == second:
                nc.scalar.copy(out_bf[:, :, t], page[t][:])
            if t == third:
                for c in range(2):
                    cols = slice(U // 2 * c, U // 2 * (c + 1))
                    nc.scalar.copy(out_bf[:, cols, t], page[t][:, cols])
        nc.scalar.copy(out_bf[:, VEC_COLS:U, last], page[last][:, VEC_COLS:U])
        nc.vector.tensor_copy(out_bf[:, 0 : U // 2, last], page[last][:, 0 : U // 2])
        nc.vector.tensor_copy(out_bf[:, U // 2 : VEC_COLS, last], page[last][:, U // 2 : VEC_COLS])

        out_codes = sb.tile([P, U], U32, name="out_codes", align_bytes=64)
        out_scales = sb.tile([P, U], U8, name="out_scales", align_bytes=64)
        out_words = words_of(out_1)
        for cols in (slice(0, U // 2), slice(U // 2, VEC_COLS), slice(VEC_COLS, U)):
            nc.vector.quantize_mx(
                out=out_codes[:, cols].bitcast(FP8X4), scales=out_scales[:, cols],
                in_=out_bf[:, cols, :].rearrange("p u t -> p (u t)"),
            )
            nc.sync.dma_start(out_words[:, cols], out_codes[:, cols].bitcast(I32))
        for q in range(4):
            queue = nc.scalar if q < 3 else nc.sync
            queue.dma_start(
                out_2[0, 4 * q : 4 * q + 4, :].bitcast(I32),
                out_scales[32 * q : 32 * q + 4, :].bitcast(I32),
            )
